import numpy as np
import ml_dtypes


def mxq(x, axis, fmt="e4m3"):
    dtype, down = {"e4m3": (ml_dtypes.float8_e4m3fn, 7), "e5m2": (ml_dtypes.float8_e5m2, 14)}[fmt]
    v = np.moveaxis(np.asarray(x, np.float32).astype(ml_dtypes.bfloat16).astype(np.float64), axis, -1)
    blocks = v.reshape(v.shape[:-1] + (-1, 32))
    amax = np.abs(blocks).max(-1, keepdims=True)
    byte = np.maximum(np.where(amax > 0, np.frexp(amax)[1] - 1 + 127, 0) - down, 1)
    scale = np.exp2(byte - 127.0)
    codes = (blocks / scale).astype(np.float32).astype(dtype).astype(np.float64)
    return np.moveaxis((codes * scale).reshape(v.shape), -1, axis)


WIDE = False


def mx_kscale(k):
    if not WIDE:
        return np.ones(k)
    levels = np.array([10, -10, 5, -5, 0])
    if k % 512:
        return np.exp2(np.random.permutation(np.resize(levels, k // 32))).repeat(32)
    a = np.empty((k // 512, 16))
    for p in range(k // 512):
        a[p, :8] = np.random.permutation(np.resize(levels, 8))
        for g in range(8):
            far = levels[np.abs(levels - a[p, g]) >= 10]
            a[p, g + 8] = far[np.random.randint(len(far))]
    return np.exp2(a.ravel()).repeat(32)


def f64(x):
    return np.asarray(x).astype(np.float64)


def striped(idx):
    return np.tile(idx.reshape(-1, 16).T, (8, 1)).astype(np.uint16)


def unstriped(offs):
    return offs[:16].T.reshape(-1).astype(np.int64)


def sigmoid(v):
    return 1.0 / (1.0 + np.exp(-np.maximum(v, -700.0)))


K, T, E, C, H, N = 1536, 768, 4, 128, 512, 128


def by_expert(wq, xq):
    return np.concatenate([wq[e].T @ xq[:, e * C:(e + 1) * C] for e in range(E)], axis=1)


def setup_inputs():
    n = np.random.standard_normal
    s = mx_kscale(K)[:, None]
    u = mx_kscale(H)
    return {
        "xT": (n((K, T)) * s).astype(np.float32),
        "w1": (n((E, K, H)) / np.sqrt(K) / s[None]).astype(np.float32),
        "w3": (n((E, K, H)) / np.sqrt(K) / s[None] * u[None, None, :]).astype(np.float32),
        "w2": (n((E, H, N)) / np.sqrt(H) / u[None, :, None]).astype(np.float32),
        "gate": np.tile(np.random.uniform(0.2, 1.0, E * C), (N, 1)).astype(np.float32),
        "offs": striped(np.random.permutation(T)[:E * C]),
    }


def reference(xT, w1, w3, w2, gate, offs):
    idx = unstriped(offs)
    xq = mxq(f64(xT)[:, idx], 0, "e4m3")
    h = sigmoid(by_expert(mxq(f64(w1), 1, "e4m3"), xq))
    h = h * by_expert(mxq(f64(w3), 1, "e4m3"), xq)
    y = by_expert(mxq(f64(w2), 1, "e4m3"), mxq(h, 0, "e4m3"))
    out = np.zeros((N, T))
    out[:, idx] = f64(gate) * y
    return out

@@ -1,0 +1,160 @@
+from contextlib import ExitStack
+
+import concourse.mybir as mybir
+
+K, T, E, C, H, N = 1536, 768, 4, 128, 512, 128
+S = E * C
+
+FLOPS = 2 * S * (2 * K * H + H * N)
+
+F32 = mybir.dt.float32
+BF16 = mybir.dt.bfloat16
+U32 = mybir.dt.uint32
+U16 = mybir.dt.uint16
+U8 = mybir.dt.uint8
+FP8X4 = mybir.dt.float8_e4m3fn_x4
+SIGMOID = mybir.ActivationFunctionType.Sigmoid
+MULT = mybir.AluOpType.mult
+
+P = 128
+PACK = 4
+K_PASS = P * PACK
+PASSES = K // K_PASS
+
+X_VECTOR = 128
+W_VECTOR = 68
+
+
+def tile_routed_moe_kernel(tc, xT, w1, w3, w2, gate, offs, out):
+    nc = tc.nc
+    with ExitStack() as ctx:
+        keep = ctx.enter_context(tc.tile_pool(name="keep", bufs=1))
+        x_stage = ctx.enter_context(tc.tile_pool(name="x_stage", bufs=2))
+        w_load = ctx.enter_context(tc.tile_pool(name="w_load", bufs=9))
+        w_stage = ctx.enter_context(tc.tile_pool(name="w_stage", bufs=4))
+        w_codes = ctx.enter_context(tc.tile_pool(name="w_codes", bufs=4))
+        hidden = ctx.enter_context(tc.tile_pool(name="hidden", bufs=2))
+        psum = ctx.enter_context(tc.psum_pool(name="psum", bufs=2))
+
+        offsets = keep.tile([P, S // 16], U16, name="offsets")
+        nc.sync.dma_start(offsets[:], offs)
+
+        warm = keep.tile([P, 1], F32, name="warm")
+        nc.vector.memset(warm[:], 0.0)
+        nc.scalar.activation(warm[:], warm[:], SIGMOID)
+
+        window = keep.tile([P, T], F32, name="window")
+        nc.vector.memset(window[:], 0.0)
+        x_scales = []
+        for g in range(PASSES):
+            plane = keep.tile([P, T], U8, name="x_scales%d" % g, align_bytes=64)
+            nc.gpsimd.memset(plane[:], 0)
+            x_scales.append(plane)
+
+        slot_codes = keep.tile([P, PASSES, S], U32, name="slot_codes", align_bytes=64)
+        slot_scales = keep.tile([P, PASSES, S], U8, name="slot_scales", align_bytes=64)
+
+        for g in range(PASSES):
+            raw = keep.tile([P, PACK, T], F32, name="x_raw%d" % g)
+            nc.sync.dma_start(out=raw[:], in_=xT[g * K_PASS : (g + 1) * K_PASS, :].rearrange("(p j) t -> p j t", j=PACK))
+            grouped = x_stage.tile([P, T, PACK], BF16, name="x_grouped", align_bytes=64)
+            nc.vector.tensor_copy(out=grouped[:, :X_VECTOR, :], in_=raw[:, :, :X_VECTOR].rearrange("p j t -> p t j"))
+            nc.scalar.copy(out=grouped[:, X_VECTOR:, :], in_=raw[:, :, X_VECTOR:].rearrange("p j t -> p t j"))
+            codes = x_stage.tile([P, T], U32, name="x_codes", align_bytes=64)
+            for lo, hi in ((0, 512), (512, T)):
+                nc.vector.quantize_mx(
+                    out=codes[:, lo:hi].bitcast(FP8X4),
+                    scales=x_scales[g][:, lo:hi],
+                    in_=grouped[:, lo:hi, :].rearrange("p t j -> p (t j)"),
+                )
+            nc.vector.tensor_copy(slot_codes[:, g, :], codes[:].indirect(offsets[:]))
+            nc.vector.tensor_copy(slot_scales[:, g, :], x_scales[g][:].indirect(offsets[:]))
+
+        w2_codes = keep.tile([P, E, N], U32, name="w2_codes", align_bytes=64)
+        w2_scales = keep.tile([P, E, N], U8, name="w2_scales", align_bytes=64)
+        gates = keep.tile([P, S], F32, name="gates")
+
+        def load_up_weights(w, e, last=False):
+            step_of = lambda g: 1 if last and g == PASSES - 1 else PACK
+            codes = w_codes.tile([P, PASSES, H], U32, name="up_codes", align_bytes=64)
+            scales = w_codes.tile([P, PASSES, H], U8, name="up_scales", align_bytes=64)
+            for g in range(PASSES):
+                raw = w_load.tile([P, PACK, H], F32, name="w_raw")
+                nc.sync.dma_start(out=raw[:], in_=w[e, g * K_PASS : (g + 1) * K_PASS, :].rearrange("(p j) i -> p j i", j=PACK))
+                grouped = w_stage.tile([P, H * PACK], BF16, name="w_grouped", align_bytes=64)
+                dst = grouped[:].rearrange("p (t m j) -> p m t j", t=PACK, j=PACK)
+                src = raw[:].rearrange("p j (m t) -> p m t j", t=PACK)
+                nc.vector.tensor_copy(out=dst[:, :W_VECTOR], in_=src[:, :W_VECTOR])
+                nc.scalar.copy(out=dst[:, W_VECTOR:], in_=src[:, W_VECTOR:])
+                for t in range(0, PACK, step_of(g)):
+                    cols = slice(t * P, (t + step_of(g)) * P)
+                    nc.vector.quantize_mx(
+                        out=codes[:, g, cols].bitcast(FP8X4),
+                        scales=scales[:, g, cols],
+                        in_=grouped[:, PACK * cols.start : PACK * cols.stop],
+                    )
+            return codes, scales
+
+        def load_down_weights(lo, hi):
+            n = hi - lo
+            raw = keep.tile([P, n, PACK, N], F32, name="w2_raw%d" % lo)
+            nc.sync.dma_start(out=raw[:], in_=w2[lo:hi].rearrange("e (p j) n -> p e (j n)", j=PACK))
+            for e in range(lo, hi):
+                grouped = w_stage.tile([P, N, PACK], BF16, name="w2_grouped", align_bytes=64)
+                nc.scalar.copy(out=grouped[:], in_=raw[:, e - lo].rearrange("p j n -> p n j"))
+                nc.vector.quantize_mx(
+                    out=w2_codes[:, e, :].bitcast(FP8X4),
+                    scales=w2_scales[:, e, :],
+                    in_=grouped[:].rearrange("p n j -> p (n j)"),
+                )
+
+        def up(codes, scales, e, name):
+            acc = psum.tile([P, PACK, C], F32, name=name)
+            slots = slice(e * C, (e + 1) * C)
+            for t in range(PACK):
+                cols = slice(t * P, (t + 1) * P)
+                for g in range(PASSES):
+                    nc.tensor.matmul_mx(
+                        out=acc[:, t, :],
+                        lhsT=codes[:, g, cols].bitcast(FP8X4),
+                        lhsT_scale=scales[:, g, cols],
+                        rhs=slot_codes[:, g, slots].bitcast(FP8X4),
+                        rhs_scale=slot_scales[:, g, slots],
+                        start=(g == 0),
+                        stop=(g == PASSES - 1),
+                    )
+            return acc
+
+        for e in range(E):
+            slots = slice(e * C, (e + 1) * C)
+            c1, s1 = load_up_weights(w1, e)
+            acc_a = up(c1, s1, e, "acc_a")
+            sig = hidden.tile([P, C, PACK], F32, name="sig")
+            nc.scalar.activation(sig[:], acc_a[:].rearrange("p t c -> p c t"), SIGMOID)
+            c3, s3 = load_up_weights(w3, e, e == E - 1)
+            acc_b = up(c3, s3, e, "acc_b")
+            if e == 0:
+                load_down_weights(0, E - 1)
+                nc.sync.dma_start(out=gates[:], in_=gate)
+            if e == E - 1:
+                load_down_weights(E - 1, E)
+            h = hidden.tile([P, C, PACK], BF16, name="h", align_bytes=64)
+            nc.vector.tensor_tensor(h[:], acc_b[:].rearrange("p t c -> p c t"), sig[:], MULT)
+            h_codes = hidden.tile([P, C], U32, name="h_codes", align_bytes=64)
+            h_scales = hidden.tile([P, C], U8, name="h_scales", align_bytes=64)
+            nc.vector.quantize_mx(out=h_codes[:].bitcast(FP8X4), scales=h_scales[:], in_=h[:].rearrange("p c t -> p (c t)"))
+            acc_y = psum.tile([P, C], F32, name="acc_y")
+            nc.tensor.matmul_mx(
+                out=acc_y[:],
+                lhsT=w2_codes[:, e, :].bitcast(FP8X4),
+                lhsT_scale=w2_scales[:, e, :],
+                rhs=h_codes[:].bitcast(FP8X4),
+                rhs_scale=h_scales[:],
+                start=True,
+                stop=True,
+            )
+            y = hidden.tile([P, C], F32, name="y")
+            nc.scalar.copy(out=y[:], in_=acc_y[:])
+            nc.vector.tensor_tensor(window[:].indirect(offsets[:, e * (C // 16) : (e + 1) * (C // 16)]), y[:], gates[:, slots], MULT)
+
+        nc.sync.dma_start(out=out, in_=window[:])

@@ -20,9 +20,14 @@ P = 128
 PACK = 4
 K_PASS = P * PACK
 PASSES = K // K_PASS
+LIST_ROWS = 16
+PLANE_STEP = 4
 
+LAST = E - 1
 X_VECTOR = 128
-W_VECTOR = 68
+W_VECTOR = 62
+W_VECTOR_END = 84
+FIRST_DOWN = 1
 
 
 def tile_routed_moe_kernel(tc, xT, w1, w3, w2, gate, offs, out):
@@ -30,13 +35,14 @@ def tile_routed_moe_kernel(tc, xT, w1, w3, w2, gate, offs, out):
     with ExitStack() as ctx:
         keep = ctx.enter_context(tc.tile_pool(name="keep", bufs=1))
         x_stage = ctx.enter_context(tc.tile_pool(name="x_stage", bufs=2))
-        w_load = ctx.enter_context(tc.tile_pool(name="w_load", bufs=9))
+        w_load = ctx.enter_context(tc.tile_pool(name="w_load", bufs=3))
         w_stage = ctx.enter_context(tc.tile_pool(name="w_stage", bufs=4))
         w_codes = ctx.enter_context(tc.tile_pool(name="w_codes", bufs=4))
         hidden = ctx.enter_context(tc.tile_pool(name="hidden", bufs=2))
-        psum = ctx.enter_context(tc.psum_pool(name="psum", bufs=2))
+        psum = ctx.enter_context(tc.psum_pool(name="psum", bufs=1))
+        psum_y = ctx.enter_context(tc.psum_pool(name="psum_y", bufs=2))
 
-        offsets = keep.tile([P, S // 16], U16, name="offsets")
+        offsets = keep.tile([P, S // LIST_ROWS], U16, name="offsets")
         nc.sync.dma_start(offsets[:], offs)
 
         warm = keep.tile([P, 1], F32, name="warm")
@@ -45,14 +51,11 @@ def tile_routed_moe_kernel(tc, xT, w1, w3, w2, gate, offs, out):
 
         window = keep.tile([P, T], F32, name="window")
         nc.vector.memset(window[:], 0.0)
-        x_scales = []
-        for g in range(PASSES):
-            plane = keep.tile([P, T], U8, name="x_scales%d" % g, align_bytes=64)
-            nc.gpsimd.memset(plane[:], 0)
-            x_scales.append(plane)
 
+        x_scales = keep.tile([P, T], U8, name="x_scales", align_bytes=64)
+        nc.gpsimd.memset(x_scales[:], 0)
         slot_codes = keep.tile([P, PASSES, S], U32, name="slot_codes", align_bytes=64)
-        slot_scales = keep.tile([P, PASSES, S], U8, name="slot_scales", align_bytes=64)
+        slot_scales = keep.tile([P, S], U8, name="slot_scales", align_bytes=64)
 
         for g in range(PASSES):
             raw = keep.tile([P, PACK, T], F32, name="x_raw%d" % g)
@@ -64,30 +67,34 @@ def tile_routed_moe_kernel(tc, xT, w1, w3, w2, gate, offs, out):
             for lo, hi in ((0, 512), (512, T)):
                 nc.vector.quantize_mx(
                     out=codes[:, lo:hi].bitcast(FP8X4),
-                    scales=x_scales[g][:, lo:hi],
+                    scales=x_scales[PLANE_STEP * g : P, lo:hi],
                     in_=grouped[:, lo:hi, :].rearrange("p t j -> p (t j)"),
                 )
             nc.vector.tensor_copy(slot_codes[:, g, :], codes[:].indirect(offsets[:]))
-            nc.vector.tensor_copy(slot_scales[:, g, :], x_scales[g][:].indirect(offsets[:]))
+        nc.vector.tensor_copy(slot_scales[:], x_scales[:].indirect(offsets[:]))
 
         w2_codes = keep.tile([P, E, N], U32, name="w2_codes", align_bytes=64)
         w2_scales = keep.tile([P, E, N], U8, name="w2_scales", align_bytes=64)
-        gates = keep.tile([P, S], F32, name="gates")
 
-        def load_up_weights(w, e, last=False):
-            step_of = lambda g: 1 if last and g == PASSES - 1 else PACK
+        def up_weights(w, e, by_pass, to_the_end=False):
             codes = w_codes.tile([P, PASSES, H], U32, name="up_codes", align_bytes=64)
             scales = w_codes.tile([P, PASSES, H], U8, name="up_scales", align_bytes=64)
+            raw = w_load.tile([P, PASSES, PACK * H], F32, name="w_raw")
+            rows = w[e].rearrange("(g p j) i -> p g (j i)", g=PASSES, j=PACK)
+            width = 1 if by_pass else PASSES
+            for g in range(0, PASSES, width):
+                nc.sync.dma_start(out=raw[:, g : g + width], in_=rows[:, g : g + width])
             for g in range(PASSES):
-                raw = w_load.tile([P, PACK, H], F32, name="w_raw")
-                nc.sync.dma_start(out=raw[:], in_=w[e, g * K_PASS : (g + 1) * K_PASS, :].rearrange("(p j) i -> p j i", j=PACK))
+                at_end = to_the_end and g == PASSES - 1
                 grouped = w_stage.tile([P, H * PACK], BF16, name="w_grouped", align_bytes=64)
                 dst = grouped[:].rearrange("p (t m j) -> p m t j", t=PACK, j=PACK)
-                src = raw[:].rearrange("p j (m t) -> p m t j", t=PACK)
-                nc.vector.tensor_copy(out=dst[:, :W_VECTOR], in_=src[:, :W_VECTOR])
-                nc.scalar.copy(out=dst[:, W_VECTOR:], in_=src[:, W_VECTOR:])
-                for t in range(0, PACK, step_of(g)):
-                    cols = slice(t * P, (t + step_of(g)) * P)
+                src = raw[:, g].rearrange("p (j m t) -> p m t j", j=PACK, t=PACK)
+                mid = W_VECTOR_END if at_end else W_VECTOR
+                nc.vector.tensor_copy(out=dst[:, :mid], in_=src[:, :mid])
+                nc.scalar.copy(out=dst[:, mid:], in_=src[:, mid:])
+                slices = 1 if at_end else PACK
+                for t in range(0, PACK, slices):
+                    cols = slice(t * P, (t + slices) * P)
                     nc.vector.quantize_mx(
                         out=codes[:, g, cols].bitcast(FP8X4),
                         scales=scales[:, g, cols],
@@ -95,66 +102,97 @@ def tile_routed_moe_kernel(tc, xT, w1, w3, w2, gate, offs, out):
                     )
             return codes, scales
 
-        def load_down_weights(lo, hi):
-            n = hi - lo
-            raw = keep.tile([P, n, PACK, N], F32, name="w2_raw%d" % lo)
-            nc.sync.dma_start(out=raw[:], in_=w2[lo:hi].rearrange("e (p j) n -> p e (j n)", j=PACK))
-            for e in range(lo, hi):
+        def down_weights(experts, raw):
+            for e in experts:
+                nc.sync.dma_start(out=raw[:, e], in_=w2[e].rearrange("(p j) n -> p (j n)", j=PACK))
+            for e in experts:
                 grouped = w_stage.tile([P, N, PACK], BF16, name="w2_grouped", align_bytes=64)
-                nc.scalar.copy(out=grouped[:], in_=raw[:, e - lo].rearrange("p j n -> p n j"))
+                nc.scalar.copy(out=grouped[:], in_=raw[:, e].rearrange("p (j n) -> p n j", j=PACK))
                 nc.vector.quantize_mx(
                     out=w2_codes[:, e, :].bitcast(FP8X4),
                     scales=w2_scales[:, e, :],
                     in_=grouped[:].rearrange("p n j -> p (n j)"),
                 )
 
-        def up(codes, scales, e, name):
-            acc = psum.tile([P, PACK, C], F32, name=name)
+        def up_slice(acc, weights, e, t, passes):
+            codes, scales = weights
             slots = slice(e * C, (e + 1) * C)
+            cols = slice(t * P, (t + 1) * P)
+            for g in passes:
+                nc.tensor.matmul_mx(
+                    out=acc,
+                    lhsT=codes[:, g, cols].bitcast(FP8X4),
+                    lhsT_scale=scales[:, g, cols],
+                    rhs=slot_codes[:, g, slots].bitcast(FP8X4),
+                    rhs_scale=slot_scales[PLANE_STEP * g : P, slots],
+                    start=(g == 0),
+                    stop=(g == PASSES - 1),
+                )
+
+        def up(weights, e, name):
+            acc = psum.tile([P, PACK, C], F32, name=name)
             for t in range(PACK):
-                cols = slice(t * P, (t + 1) * P)
-                for g in range(PASSES):
-                    nc.tensor.matmul_mx(
-                        out=acc[:, t, :],
-                        lhsT=codes[:, g, cols].bitcast(FP8X4),
-                        lhsT_scale=scales[:, g, cols],
-                        rhs=slot_codes[:, g, slots].bitcast(FP8X4),
-                        rhs_scale=slot_scales[:, g, slots],
-                        start=(g == 0),
-                        stop=(g == PASSES - 1),
-                    )
+                up_slice(acc[:, t, :], weights, e, t, range(PASSES))
             return acc
 
-        for e in range(E):
-            slots = slice(e * C, (e + 1) * C)
-            c1, s1 = load_up_weights(w1, e)
-            acc_a = up(c1, s1, e, "acc_a")
-            sig = hidden.tile([P, C, PACK], F32, name="sig")
-            nc.scalar.activation(sig[:], acc_a[:].rearrange("p t c -> p c t"), SIGMOID)
-            c3, s3 = load_up_weights(w3, e, e == E - 1)
-            acc_b = up(c3, s3, e, "acc_b")
-            if e == 0:
-                load_down_weights(0, E - 1)
-                nc.sync.dma_start(out=gates[:], in_=gate)
-            if e == E - 1:
-                load_down_weights(E - 1, E)
-            h = hidden.tile([P, C, PACK], BF16, name="h", align_bytes=64)
-            nc.vector.tensor_tensor(h[:], acc_b[:].rearrange("p t c -> p c t"), sig[:], MULT)
-            h_codes = hidden.tile([P, C], U32, name="h_codes", align_bytes=64)
-            h_scales = hidden.tile([P, C], U8, name="h_scales", align_bytes=64)
-            nc.vector.quantize_mx(out=h_codes[:].bitcast(FP8X4), scales=h_scales[:], in_=h[:].rearrange("p c t -> p (c t)"))
-            acc_y = psum.tile([P, C], F32, name="acc_y")
+        hidden_codes = []
+
+        def quantise_hidden(e, h):
+            codes = keep.tile([P, C], U32, name="h_codes%d" % e, align_bytes=64)
+            scales = keep.tile([P, C], U8, name="h_scales%d" % e, align_bytes=64)
+            nc.vector.quantize_mx(out=codes[:].bitcast(FP8X4), scales=scales[:], in_=h[:].rearrange("p c t -> p (c t)"))
+            hidden_codes.append((codes, scales))
+
+        def down(e, gates):
+            codes, scales = hidden_codes[e]
+            acc_y = psum_y.tile([P, C], F32, name="acc_y")
             nc.tensor.matmul_mx(
                 out=acc_y[:],
                 lhsT=w2_codes[:, e, :].bitcast(FP8X4),
                 lhsT_scale=w2_scales[:, e, :],
-                rhs=h_codes[:].bitcast(FP8X4),
-                rhs_scale=h_scales[:],
+                rhs=codes[:].bitcast(FP8X4),
+                rhs_scale=scales[:],
                 start=True,
                 stop=True,
             )
             y = hidden.tile([P, C], F32, name="y")
             nc.scalar.copy(out=y[:], in_=acc_y[:])
-            nc.vector.tensor_tensor(window[:].indirect(offsets[:, e * (C // 16) : (e + 1) * (C // 16)]), y[:], gates[:, slots], MULT)
+            entries = offsets[:, e * C // LIST_ROWS : (e + 1) * C // LIST_ROWS]
+            nc.vector.tensor_tensor(window[:].indirect(entries), y[:], gates[:, e * C : (e + 1) * C], MULT)
+
+        gates = keep.tile([P, S], F32, name="gates")
+        for e in range(LAST):
+            acc_a = up(up_weights(w1, e, by_pass=False), e, "acc_a")
+            sig = hidden.tile([P, C, PACK], F32, name="sig")
+            nc.scalar.activation(sig[:], acc_a[:].rearrange("p t c -> p c t"), SIGMOID)
+            acc_b = up(up_weights(w3, e, by_pass=(e == LAST - 1)), e, "acc_b")
+            if e == 0:
+                w2_early = keep.tile([P, FIRST_DOWN, PACK * N], F32, name="w2_early")
+                down_weights(range(FIRST_DOWN), w2_early)
+                nc.sync.dma_start(out=gates[:], in_=gate)
+            h = hidden.tile([P, C, PACK], BF16, name="h", align_bytes=64)
+            nc.vector.tensor_tensor(h[:], acc_b[:].rearrange("p t c -> p c t"), sig[:], MULT)
+            quantise_hidden(e, h)
+            if e < FIRST_DOWN:
+                down(e, gates)
+
+        acc_a = up(up_weights(w1, LAST, by_pass=True), LAST, "acc_a")
+        sig = hidden.tile([P, PACK, C], F32, name="sig")
+        nc.scalar.activation(sig[:], acc_a[:], SIGMOID)
+        weights = up_weights(w3, LAST, by_pass=True, to_the_end=True)
+        acc_last = [psum.tile([P, PACK, C], F32, name="acc_last%d" % t) for t in range(PACK)]
+        for passes in (range(PASSES - 1), range(PASSES - 1, PASSES)):
+            for t in range(PACK):
+                up_slice(acc_last[t][:, 0, :], weights, LAST, t, passes)
+        w2_late = w_load.tile([P, E, PACK * N], F32, name="w_raw")
+        down_weights(range(FIRST_DOWN, E), w2_late)
+        planes = hidden.tile([P, PACK, C], F32, name="h_planes", bufs=1)
+        for t in range(PACK):
+            nc.vector.tensor_tensor(planes[:, t, :], acc_last[t][:, 0, :], sig[:, t, :], MULT)
+        h = hidden.tile([P, C, PACK], BF16, name="h", align_bytes=64)
+        nc.vector.tensor_copy(out=h[:], in_=planes[:].rearrange("p t c -> p c t"))
+        quantise_hidden(LAST, h)
+        for e in range(FIRST_DOWN, E):
+            down(e, gates)
 
         nc.sync.dma_start(out=out, in_=window[:])

from contextlib import ExitStack

import concourse.mybir as mybir

K, T, E, C, H, N = 1536, 768, 4, 128, 512, 128
S = E * C

FLOPS = 2 * S * (2 * K * H + H * N)

F32 = mybir.dt.float32
BF16 = mybir.dt.bfloat16
U32 = mybir.dt.uint32
U16 = mybir.dt.uint16
U8 = mybir.dt.uint8
FP8X4 = mybir.dt.float8_e4m3fn_x4
SIGMOID = mybir.ActivationFunctionType.Sigmoid
MULT = mybir.AluOpType.mult

P = 128
PACK = 4
K_PASS = P * PACK
PASSES = K // K_PASS
LIST_ROWS = 16
PLANE_STEP = 4

LAST = E - 1
X_VECTOR = 128
W_VECTOR = 62
W_VECTOR_END = 84
FIRST_DOWN = 1


def tile_routed_moe_kernel(tc, xT, w1, w3, w2, gate, offs, out):
    nc = tc.nc
    with ExitStack() as ctx:
        keep = ctx.enter_context(tc.tile_pool(name="keep", bufs=1))
        x_stage = ctx.enter_context(tc.tile_pool(name="x_stage", bufs=2))
        w_load = ctx.enter_context(tc.tile_pool(name="w_load", bufs=3))
        w_stage = ctx.enter_context(tc.tile_pool(name="w_stage", bufs=4))
        w_codes = ctx.enter_context(tc.tile_pool(name="w_codes", bufs=4))
        hidden = ctx.enter_context(tc.tile_pool(name="hidden", bufs=2))
        psum = ctx.enter_context(tc.psum_pool(name="psum", bufs=1))
        psum_y = ctx.enter_context(tc.psum_pool(name="psum_y", bufs=2))

        offsets = keep.tile([P, S // LIST_ROWS], U16, name="offsets")
        nc.sync.dma_start(offsets[:], offs)

        warm = keep.tile([P, 1], F32, name="warm")
        nc.vector.memset(warm[:], 0.0)
        nc.scalar.activation(warm[:], warm[:], SIGMOID)

        window = keep.tile([P, T], F32, name="window")
        nc.vector.memset(window[:], 0.0)

        x_scales = keep.tile([P, T], U8, name="x_scales", align_bytes=64)
        nc.gpsimd.memset(x_scales[:], 0)
        slot_codes = keep.tile([P, PASSES, S], U32, name="slot_codes", align_bytes=64)
        slot_scales = keep.tile([P, S], U8, name="slot_scales", align_bytes=64)

        for g in range(PASSES):
            raw = keep.tile([P, PACK, T], F32, name="x_raw%d" % g)
            nc.sync.dma_start(out=raw[:], in_=xT[g * K_PASS : (g + 1) * K_PASS, :].rearrange("(p j) t -> p j t", j=PACK))
            grouped = x_stage.tile([P, T, PACK], BF16, name="x_grouped", align_bytes=64)
            nc.vector.tensor_copy(out=grouped[:, :X_VECTOR, :], in_=raw[:, :, :X_VECTOR].rearrange("p j t -> p t j"))
            nc.scalar.copy(out=grouped[:, X_VECTOR:, :], in_=raw[:, :, X_VECTOR:].rearrange("p j t -> p t j"))
            codes = x_stage.tile([P, T], U32, name="x_codes", align_bytes=64)
            for lo, hi in ((0, 512), (512, T)):
                nc.vector.quantize_mx(
                    out=codes[:, lo:hi].bitcast(FP8X4),
                    scales=x_scales[PLANE_STEP * g : P, lo:hi],
                    in_=grouped[:, lo:hi, :].rearrange("p t j -> p (t j)"),
                )
            nc.vector.tensor_copy(slot_codes[:, g, :], codes[:].indirect(offsets[:]))
        nc.vector.tensor_copy(slot_scales[:], x_scales[:].indirect(offsets[:]))

        w2_codes = keep.tile([P, E, N], U32, name="w2_codes", align_bytes=64)
        w2_scales = keep.tile([P, E, N], U8, name="w2_scales", align_bytes=64)

        def up_weights(w, e, by_pass, to_the_end=False):
            codes = w_codes.tile([P, PASSES, H], U32, name="up_codes", align_bytes=64)
            scales = w_codes.tile([P, PASSES, H], U8, name="up_scales", align_bytes=64)
            raw = w_load.tile([P, PASSES, PACK * H], F32, name="w_raw")
            rows = w[e].rearrange("(g p j) i -> p g (j i)", g=PASSES, j=PACK)
            width = 1 if by_pass else PASSES
            for g in range(0, PASSES, width):
                nc.sync.dma_start(out=raw[:, g : g + width], in_=rows[:, g : g + width])
            for g in range(PASSES):
                at_end = to_the_end and g == PASSES - 1
                grouped = w_stage.tile([P, H * PACK], BF16, name="w_grouped", align_bytes=64)
                dst = grouped[:].rearrange("p (t m j) -> p m t j", t=PACK, j=PACK)
                src = raw[:, g].rearrange("p (j m t) -> p m t j", j=PACK, t=PACK)
                mid = W_VECTOR_END if at_end else W_VECTOR
                nc.vector.tensor_copy(out=dst[:, :mid], in_=src[:, :mid])
                nc.scalar.copy(out=dst[:, mid:], in_=src[:, mid:])
                slices = 1 if at_end else PACK
                for t in range(0, PACK, slices):
                    cols = slice(t * P, (t + slices) * P)
                    nc.vector.quantize_mx(
                        out=codes[:, g, cols].bitcast(FP8X4),
                        scales=scales[:, g, cols],
                        in_=grouped[:, PACK * cols.start : PACK * cols.stop],
                    )
            return codes, scales

        def down_weights(experts, raw):
            for e in experts:
                nc.sync.dma_start(out=raw[:, e], in_=w2[e].rearrange("(p j) n -> p (j n)", j=PACK))
            for e in experts:
                grouped = w_stage.tile([P, N, PACK], BF16, name="w2_grouped", align_bytes=64)
                nc.scalar.copy(out=grouped[:], in_=raw[:, e].rearrange("p (j n) -> p n j", j=PACK))
                nc.vector.quantize_mx(
                    out=w2_codes[:, e, :].bitcast(FP8X4),
                    scales=w2_scales[:, e, :],
                    in_=grouped[:].rearrange("p n j -> p (n j)"),
                )

        def up_slice(acc, weights, e, t, passes):
            codes, scales = weights
            slots = slice(e * C, (e + 1) * C)
            cols = slice(t * P, (t + 1) * P)
            for g in passes:
                nc.tensor.matmul_mx(
                    out=acc,
                    lhsT=codes[:, g, cols].bitcast(FP8X4),
                    lhsT_scale=scales[:, g, cols],
                    rhs=slot_codes[:, g, slots].bitcast(FP8X4),
                    rhs_scale=slot_scales[PLANE_STEP * g : P, slots],
                    start=(g == 0),
                    stop=(g == PASSES - 1),
                )

        def up(weights, e, name):
            acc = psum.tile([P, PACK, C], F32, name=name)
            for t in range(PACK):
                up_slice(acc[:, t, :], weights, e, t, range(PASSES))
            return acc

        hidden_codes = []

        def quantise_hidden(e, h):
            codes = keep.tile([P, C], U32, name="h_codes%d" % e, align_bytes=64)
            scales = keep.tile([P, C], U8, name="h_scales%d" % e, align_bytes=64)
            nc.vector.quantize_mx(out=codes[:].bitcast(FP8X4), scales=scales[:], in_=h[:].rearrange("p c t -> p (c t)"))
            hidden_codes.append((codes, scales))

        def down(e, gates):
            codes, scales = hidden_codes[e]
            acc_y = psum_y.tile([P, C], F32, name="acc_y")
            nc.tensor.matmul_mx(
                out=acc_y[:],
                lhsT=w2_codes[:, e, :].bitcast(FP8X4),
                lhsT_scale=w2_scales[:, e, :],
                rhs=codes[:].bitcast(FP8X4),
                rhs_scale=scales[:],
                start=True,
                stop=True,
            )
            y = hidden.tile([P, C], F32, name="y")
            nc.scalar.copy(out=y[:], in_=acc_y[:])
            entries = offsets[:, e * C // LIST_ROWS : (e + 1) * C // LIST_ROWS]
            nc.vector.tensor_tensor(window[:].indirect(entries), y[:], gates[:, e * C : (e + 1) * C], MULT)

        gates = keep.tile([P, S], F32, name="gates")
        for e in range(LAST):
            acc_a = up(up_weights(w1, e, by_pass=False), e, "acc_a")
            sig = hidden.tile([P, C, PACK], F32, name="sig")
            nc.scalar.activation(sig[:], acc_a[:].rearrange("p t c -> p c t"), SIGMOID)
            acc_b = up(up_weights(w3, e, by_pass=(e == LAST - 1)), e, "acc_b")
            if e == 0:
                w2_early = keep.tile([P, FIRST_DOWN, PACK * N], F32, name="w2_early")
                down_weights(range(FIRST_DOWN), w2_early)
                nc.sync.dma_start(out=gates[:], in_=gate)
            h = hidden.tile([P, C, PACK], BF16, name="h", align_bytes=64)
            nc.vector.tensor_tensor(h[:], acc_b[:].rearrange("p t c -> p c t"), sig[:], MULT)
            quantise_hidden(e, h)
            if e < FIRST_DOWN:
                down(e, gates)

        acc_a = up(up_weights(w1, LAST, by_pass=True), LAST, "acc_a")
        sig = hidden.tile([P, PACK, C], F32, name="sig")
        nc.scalar.activation(sig[:], acc_a[:], SIGMOID)
        weights = up_weights(w3, LAST, by_pass=True, to_the_end=True)
        acc_last = [psum.tile([P, PACK, C], F32, name="acc_last%d" % t) for t in range(PACK)]
        for passes in (range(PASSES - 1), range(PASSES - 1, PASSES)):
            for t in range(PACK):
                up_slice(acc_last[t][:, 0, :], weights, LAST, t, passes)
        w2_late = w_load.tile([P, E, PACK * N], F32, name="w_raw")
        down_weights(range(FIRST_DOWN, E), w2_late)
        planes = hidden.tile([P, PACK, C], F32, name="h_planes", bufs=1)
        for t in range(PACK):
            nc.vector.tensor_tensor(planes[:, t, :], acc_last[t][:, 0, :], sig[:, t, :], MULT)
        h = hidden.tile([P, C, PACK], BF16, name="h", align_bytes=64)
        nc.vector.tensor_copy(out=h[:], in_=planes[:].rearrange("p t c -> p c t"))
        quantise_hidden(LAST, h)
        for e in range(FIRST_DOWN, E):
            down(e, gates)

        nc.sync.dma_start(out=out, in_=window[:])
